import numpy as np
import ml_dtypes


def mxq(x, axis, fmt="e4m3"):
    dtype, down = {"e4m3": (ml_dtypes.float8_e4m3fn, 7), "e5m2": (ml_dtypes.float8_e5m2, 14)}[fmt]
    v = np.moveaxis(np.asarray(x, np.float32).astype(ml_dtypes.bfloat16).astype(np.float64), axis, -1)
    blocks = v.reshape(v.shape[:-1] + (-1, 32))
    amax = np.abs(blocks).max(-1, keepdims=True)
    byte = np.maximum(np.where(amax > 0, np.frexp(amax)[1] - 1 + 127, 0) - down, 1)
    scale = np.exp2(byte - 127.0)
    codes = (blocks / scale).astype(np.float32).astype(dtype).astype(np.float64)
    return np.moveaxis((codes * scale).reshape(v.shape), -1, axis)


WIDE = False


def mx_kscale(k):
    if not WIDE:
        return np.ones(k)
    levels = np.array([10, -10, 5, -5, 0])
    if k % 512:
        return np.exp2(np.random.permutation(np.resize(levels, k // 32))).repeat(32)
    a = np.empty((k // 512, 16))
    for p in range(k // 512):
        a[p, :8] = np.random.permutation(np.resize(levels, 8))
        for g in range(8):
            far = levels[np.abs(levels - a[p, g]) >= 10]
            a[p, g + 8] = far[np.random.randint(len(far))]
    return np.exp2(a.ravel()).repeat(32)


def f64(x):
    return np.asarray(x).astype(np.float64)


def striped(idx):
    return np.tile(idx.reshape(-1, 16).T, (8, 1)).astype(np.uint16)


def unstriped(offs):
    return offs[:16].T.reshape(-1).astype(np.int64)


def silu(v):
    return v / (1.0 + np.exp(-np.maximum(v, -700.0)))


K, T, D, S, V, H, N = 512, 1024, 3, 512, 256, 512, 256


def setup_inputs():
    n = np.random.standard_normal
    s = mx_kscale(K)[:, None]
    u = mx_kscale(H)
    return {
        "xT": (n((K, T)) * s).astype(np.float32),
        "w1": (n((K, H)) / np.sqrt(K) / s * u).astype(np.float32),
        "w2": (n((H, N)) / np.sqrt(H) / u[:, None]).astype(np.float32),
        "gate": np.tile(np.random.uniform(0.2, 1.0, (D, 1, V)) / np.sqrt(D), (1, N, 1)).astype(np.float32),
        "offs": striped(np.random.permutation(T)[:S]),
        "pos1": striped(np.random.permutation(S)[:V]),
        "pos2": striped(np.random.permutation(S)[:V]),
        "pos3": striped(np.random.permutation(S)[:V]),
    }


def reference(xT, w1, w2, gate, offs, pos1, pos2, pos3):
    idx = unstriped(offs)
    xq = mxq(f64(xT)[:, idx], 0, "e4m3")
    h = silu(mxq(f64(w1), 0, "e4m3").T @ xq)
    y = mxq(f64(w2), 0, "e4m3").T @ mxq(h, 0, "e4m3")
    return sum(f64(gate[d]) * y[:, unstriped(p)] for d, p in enumerate((pos1, pos2, pos3)))

@@ -1,0 +1,227 @@
+from contextlib import ExitStack
+
+import concourse.mybir as mybir
+
+K, T, D, S, V, H, N = 512, 1024, 3, 512, 256, 512, 256
+FLOPS = 2 * S * (K * H + H * N) + 2 * D * N * V
+
+F32 = mybir.dt.float32
+BF16 = mybir.dt.bfloat16
+U32 = mybir.dt.uint32
+U16 = mybir.dt.uint16
+U8 = mybir.dt.uint8
+FP8X4 = mybir.dt.float8_e4m3fn_x4
+SILU = mybir.ActivationFunctionType.Silu
+MULT = mybir.AluOpType.mult
+ADD = mybir.AluOpType.add
+
+P = 128
+PACK = 4
+
+
+def tile_picked_sub_mlp_silu_sub_e_kernel(tc, xT, w1, w2, gate, offs, pos1, pos2, pos3, out):
+    nc = tc.nc
+    with ExitStack() as ctx:
+        keep = ctx.enter_context(tc.tile_pool(name="keep", bufs=1))
+        psum = ctx.enter_context(tc.psum_pool(name="psum", bufs=1))
+
+        offs_t = keep.tile([P, S // 16], U16, name="offs_t")
+        pos_t = [keep.tile([P, V // 16], U16, name=f"pos_t{d}") for d in range(D)]
+
+        x_rows = xT.rearrange("(p j) t -> p j t", j=PACK)
+        w1_rows = w1.rearrange("(p j) c -> p j c", j=PACK)
+        w2_rows = w2.rearrange("(p j) n -> p j n", j=PACK)
+        TH = T // 2
+        x_raw = {}
+
+        def load_x(u, h):
+            r = keep.tile([P, 2, TH], F32, name=f"x_raw{u}{h}")
+            nc.sync.dma_start(out=r[:], in_=x_rows[:, 2 * u : 2 * u + 2, h * TH : (h + 1) * TH])
+            x_raw[u, h] = r
+
+        load_x(0, 0)
+        load_x(0, 1)
+        nc.sync.dma_start(offs_t[:], offs)
+        load_x(1, 0)
+        load_x(1, 1)
+        W1_CUTS = [(0, 256), (256, 384), (384, 512)]
+        w1_raw = []
+        for a, b in W1_CUTS:
+            r = keep.tile([P, PACK, b - a], F32, name=f"w1_raw{a}")
+            nc.sync.dma_start(out=r[:], in_=w1_rows[:, :, a:b])
+            w1_raw.append(r)
+        w2_raw = keep.tile([P, PACK, N], F32, name="w2_raw")
+        nc.sync.dma_start(out=w2_raw[:], in_=w2_rows)
+        for d, p in enumerate((pos1, pos2, pos3)):
+            nc.sync.dma_start(pos_t[d][:], p)
+        gate_t = keep.tile([P, 2 * D, V], F32, name="gate_t")
+        nc.sync.dma_start(out=gate_t[:], in_=gate.rearrange("d (h p) v -> p (d h) v", p=P))
+
+        warm = keep.tile([P, 1], F32, name="warm")
+        warm_o = keep.tile([P, 1], F32, name="warm_o")
+        nc.vector.memset(warm[:], 0.0)
+        nc.scalar.activation(warm_o[:], warm[:], SILU)
+
+        x_pair = [keep.tile([P, T, 2], BF16, name=f"x_pair{u}") for u in range(2)]
+        X_VECTOR = {(0, 0): 320, (0, 1): 320, (1, 0): 0, (1, 1): 320}
+
+        def cast_x(u, h):
+            src = x_raw[u, h][:].rearrange("p e (c i) -> p c e i", i=4)
+            dst = x_pair[u][:, h * TH : (h + 1) * TH, :].rearrange("p (c i) e -> p c e i", i=4)
+            cut = X_VECTOR[u, h] // 4
+            if cut:
+                nc.vector.tensor_copy(out=dst[:, :cut], in_=src[:, :cut])
+            nc.scalar.copy(out=dst[:, cut:], in_=src[:, cut:])
+
+        xg = keep.tile([P, S, PACK], BF16, name="xg", align_bytes=64)
+        xg_words = xg[:].rearrange("p s t -> p (s t)").bitcast(U32).rearrange("p (s u) -> p s u", u=2)
+        x_codes = keep.tile([P, S], U32, name="x_codes", align_bytes=64)
+        x_scales = keep.tile([P, S], U8, name="x_scales", align_bytes=64)
+
+        def gather_x(u, a, b):
+            window = x_pair[u][:].rearrange("p t e -> p (t e)").bitcast(U32)
+            nc.vector.tensor_copy(out=xg_words[:, a:b, u], in_=window.indirect(offs_t[:, a // 16 : b // 16]))
+
+        def quant_x(a, b):
+            nc.vector.quantize_mx(
+                out=x_codes[:, a:b].bitcast(FP8X4),
+                scales=x_scales[:, a:b],
+                in_=xg[:, a:b, :].rearrange("p s t -> p (s t)"),
+            )
+
+        w1g = keep.tile([P, PACK, P, PACK], BF16, name="w1g", align_bytes=64)
+        w1_codes = keep.tile([P, H], U32, name="w1_codes", align_bytes=64)
+        w1_scales = keep.tile([P, H], U8, name="w1_scales", align_bytes=64)
+
+        def cast_w1(i, engine_copy, f0, f1):
+            a, b = W1_CUTS[i]
+            src = w1_raw[i][:].rearrange("p j (m t) -> p m j t", t=PACK)
+            n = (b - a) // PACK
+            m0, m1 = int(n * f0), int(n * f1)
+            engine_copy(
+                out=w1g[:].rearrange("p t m j -> p m j t")[:, a // PACK + m0 : a // PACK + m1],
+                in_=src[:, m0:m1],
+            )
+
+        def quant_w1(t0, t1):
+            nc.vector.quantize_mx(
+                out=w1_codes[:, t0 * P : t1 * P].bitcast(FP8X4),
+                scales=w1_scales[:, t0 * P : t1 * P],
+                in_=w1g[:, t0:t1, :, :].rearrange("p t m j -> p (t m j)"),
+            )
+
+        cast_x(0, 0)
+        cast_x(0, 1)
+        gather_x(0, 0, S)
+        cast_x(1, 0)
+        cast_x(1, 1)
+        gather_x(1, 0, S // 2)
+        gather_x(1, S // 2, S)
+        cast_w1(0, nc.scalar.copy, 0.0, 1.0)
+        cast_w1(1, nc.vector.tensor_copy, 0.0, 1.0)
+        cast_w1(2, nc.vector.tensor_copy, 0.0, 0.5)
+        cast_w1(2, nc.scalar.copy, 0.5, 1.0)
+        quant_x(0, S // 2)
+        quant_w1(0, 2)
+        quant_w1(2, 4)
+        quant_x(S // 2, S)
+
+        w2g = keep.tile([P, N, PACK], BF16, name="w2g", align_bytes=64)
+        w2_codes = keep.tile([P, N], U32, name="w2_codes", align_bytes=64)
+        w2_scales = keep.tile([P, N], U8, name="w2_scales", align_bytes=64)
+        nc.vector.tensor_copy(
+            out=w2g[:].rearrange("p (c i) j -> p c j i", i=4), in_=w2_raw[:].rearrange("p j (c i) -> p c j i", i=4)
+        )
+        nc.vector.quantize_mx(
+            out=w2_codes[:].bitcast(FP8X4), scales=w2_scales[:], in_=w2g[:].rearrange("p n j -> p (n j)")
+        )
+
+        CUTS = [(0, 128), (128, 256), (256, 384), (384, 448), (448, 512)]
+        h_codes = keep.tile([P, S], U32, name="h_codes", align_bytes=64)
+        h_scales = keep.tile([P, S], U8, name="h_scales", align_bytes=64)
+        hg = [keep.tile([P, b - a, PACK], BF16, name=f"hg{a}", align_bytes=64) for a, b in CUTS]
+        y_t = [keep.tile([P, S], F32, name=f"y_t{h}") for h in range(2)]
+
+        def layer1(c):
+            a, b = CUTS[c]
+            ps = psum.tile([P, PACK, b - a], F32, name=f"h_ps{c}", tag=f"h_ps{c % 4}")
+            for t in range(PACK):
+                nc.tensor.matmul_mx(
+                    out=ps[:, t, :],
+                    lhsT=w1_codes[:, t * P : (t + 1) * P].bitcast(FP8X4),
+                    lhsT_scale=w1_scales[:, t * P : (t + 1) * P],
+                    rhs=x_codes[:, a:b].bitcast(FP8X4),
+                    rhs_scale=x_scales[:, a:b],
+                    start=True,
+                    stop=True,
+                )
+            nc.scalar.activation(hg[c][:], ps[:].rearrange("p t s -> p s t"), SILU)
+
+        def quant_h(c):
+            a, b = CUTS[c]
+            nc.vector.quantize_mx(
+                out=h_codes[:, a:b].bitcast(FP8X4),
+                scales=h_scales[:, a:b],
+                in_=hg[c][:].rearrange("p s t -> p (s t)"),
+            )
+
+        def layer2(dst, h, a, b):
+            nc.tensor.matmul_mx(
+                out=dst,
+                lhsT=w2_codes[:, h * P : (h + 1) * P].bitcast(FP8X4),
+                lhsT_scale=w2_scales[:, h * P : (h + 1) * P],
+                rhs=h_codes[:, a:b].bitcast(FP8X4),
+                rhs_scale=h_scales[:, a:b],
+                start=True,
+                stop=True,
+            )
+
+        for c in range(5):
+            layer1(c)
+        y_a = psum.tile([P, 2, 256], F32, name="y_a")
+        y_b = psum.tile([P, 2, 192], F32, name="y_b")
+        y_c = [psum.tile([P, 64], F32, name=f"y_c{h}") for h in range(2)]
+        quant_h(0)
+        quant_h(1)
+        for h in range(2):
+            layer2(y_a[:, h, :], h, 0, 256)
+        quant_h(2)
+        for h in range(2):
+            layer2(y_b[:, h, 0:128], h, 256, 384)
+        for h in range(2):
+            nc.vector.tensor_copy(out=y_t[h][:, 0:256], in_=y_a[:, h, :])
+        quant_h(3)
+        for h in range(2):
+            layer2(y_b[:, h, 128:192], h, 384, 448)
+        quant_h(4)
+        for h in range(2):
+            layer2(y_c[h][:], h, 448, 512)
+        for h in range(2):
+            nc.vector.tensor_copy(out=y_t[h][:, 256:448], in_=y_b[:, h, :])
+        nc.vector.tensor_copy(out=y_t[1][:, 448:512], in_=y_c[1][:])
+        nc.scalar.copy(out=y_t[0][:, 448:512], in_=y_c[0][:])
+
+        prod = {}
+
+        def fetch(h, d):
+            r = keep.tile([P, V], F32, name=f"prod{h}{d}")
+            nc.vector.tensor_tensor(r[:], y_t[h][:].indirect(pos_t[d][:]), gate_t[:, 2 * d + h, :], MULT)
+            prod[h, d] = r[:]
+
+        def add(a, b, name):
+            r = keep.tile([P, V], F32, name=name)
+            nc.vector.tensor_tensor(r[:], a, b, ADD)
+            return r[:]
+
+        fetch(1, 0)
+        fetch(1, 1)
+        fetch(0, 0)
+        part1 = add(prod[1, 0], prod[1, 1], "part1")
+        fetch(0, 1)
+        fetch(1, 2)
+        part0 = add(prod[0, 0], prod[0, 1], "part0")
+        fetch(0, 2)
+        res1 = add(part1, prod[1, 2], "res1")
+        nc.sync.dma_start(out=out[P : 2 * P, :], in_=res1)
+        res0 = add(part0, prod[0, 2], "res0")
+        nc.sync.dma_start(out=out[0:P, :], in_=res0)

@@ -34,16 +34,15 @@ def tile_picked_sub_mlp_silu_sub_e_kernel(tc, xT, w1, w2, gate, offs, pos1, pos2
         TH = T // 2
         x_raw = {}
 
-        def load_x(u, h):
-            r = keep.tile([P, 2, TH], F32, name=f"x_raw{u}{h}")
-            nc.sync.dma_start(out=r[:], in_=x_rows[:, 2 * u : 2 * u + 2, h * TH : (h + 1) * TH])
-            x_raw[u, h] = r
-
-        load_x(0, 0)
-        load_x(0, 1)
+        x_raw0 = keep.tile([P, 2, T], F32, name="x_raw0")
+        nc.sync.dma_start(out=x_raw0[:], in_=x_rows[:, 0:2, :])
+        for h in range(2):
+            x_raw[0, h] = x_raw0[:, :, h * TH : (h + 1) * TH]
         nc.sync.dma_start(offs_t[:], offs)
-        load_x(1, 0)
-        load_x(1, 1)
+        for h in range(2):
+            x_raw1 = keep.tile([P, 2, TH], F32, name=f"x_raw1{h}")
+            nc.sync.dma_start(out=x_raw1[:], in_=x_rows[:, 2:4, h * TH : (h + 1) * TH])
+            x_raw[1, h] = x_raw1[:]
         W1_CUTS = [(0, 256), (256, 384), (384, 512)]
         w1_raw = []
         for a, b in W1_CUTS:
@@ -66,7 +65,7 @@ def tile_picked_sub_mlp_silu_sub_e_kernel(tc, xT, w1, w2, gate, offs, pos1, pos2
         X_VECTOR = {(0, 0): 320, (0, 1): 320, (1, 0): 0, (1, 1): 320}
 
         def cast_x(u, h):
-            src = x_raw[u, h][:].rearrange("p e (c i) -> p c e i", i=4)
+            src = x_raw[u, h].rearrange("p e (c i) -> p c e i", i=4)
             dst = x_pair[u][:, h * TH : (h + 1) * TH, :].rearrange("p (c i) e -> p c e i", i=4)
             cut = X_VECTOR[u, h] // 4
             if cut:
@@ -103,12 +102,15 @@ def tile_picked_sub_mlp_silu_sub_e_kernel(tc, xT, w1, w2, gate, offs, pos1, pos2
                 in_=src[:, m0:m1],
             )
 
-        def quant_w1(t0, t1):
-            nc.vector.quantize_mx(
-                out=w1_codes[:, t0 * P : t1 * P].bitcast(FP8X4),
-                scales=w1_scales[:, t0 * P : t1 * P],
-                in_=w1g[:, t0:t1, :, :].rearrange("p t m j -> p (t m j)"),
-            )
+        def quant_w1(half):
+            for t in range(PACK):
+                m0 = half * 64
+                cols = slice(t * P + m0, t * P + m0 + 64)
+                nc.vector.quantize_mx(
+                    out=w1_codes[:, cols].bitcast(FP8X4),
+                    scales=w1_scales[:, cols],
+                    in_=w1g[:, t, m0 : m0 + 64, :].rearrange("p m j -> p (m j)"),
+                )
 
         cast_x(0, 0)
         cast_x(0, 1)
@@ -119,11 +121,11 @@ def tile_picked_sub_mlp_silu_sub_e_kernel(tc, xT, w1, w2, gate, offs, pos1, pos2
         gather_x(1, S // 2, S)
         cast_w1(0, nc.scalar.copy, 0.0, 1.0)
         cast_w1(1, nc.vector.tensor_copy, 0.0, 1.0)
+        quant_x(0, S // 2)
+        quant_w1(0)
         cast_w1(2, nc.vector.tensor_copy, 0.0, 0.5)
         cast_w1(2, nc.scalar.copy, 0.5, 1.0)
-        quant_x(0, S // 2)
-        quant_w1(0, 2)
-        quant_w1(2, 4)
+        quant_w1(1)
         quant_x(S // 2, S)
 
         w2g = keep.tile([P, N, PACK], BF16, name="w2g", align_bytes=64)

@@ -120,13 +120,13 @@ def tile_picked_sub_mlp_silu_sub_e_kernel(tc, xT, w1, w2, gate, offs, pos1, pos2
         gather_x(1, 0, S // 2)
         gather_x(1, S // 2, S)
         cast_w1(0, nc.scalar.copy, 0.0, 1.0)
-        cast_w1(1, nc.vector.tensor_copy, 0.0, 1.0)
-        quant_x(0, S // 2)
+        cast_w1(1, nc.scalar.copy, 0.0, 1.0)
         quant_w1(0)
-        cast_w1(2, nc.vector.tensor_copy, 0.0, 0.5)
-        cast_w1(2, nc.scalar.copy, 0.5, 1.0)
+        cast_w1(2, nc.vector.tensor_copy, 0.0, 1.0)
+        quant_x(0, 128)
         quant_w1(1)
-        quant_x(S // 2, S)
+        quant_x(128, 256)
+        quant_x(256, 512)
 
         w2g = keep.tile([P, N, PACK], BF16, name="w2g", align_bytes=64)
         w2_codes = keep.tile([P, N], U32, name="w2_codes", align_bytes=64)
@@ -196,34 +196,33 @@ def tile_picked_sub_mlp_silu_sub_e_kernel(tc, xT, w1, w2, gate, offs, pos1, pos2
         for h in range(2):
             layer2(y_b[:, h, 128:192], h, 384, 448)
         quant_h(4)
-        for h in range(2):
+        for h in (1, 0):
             layer2(y_c[h][:], h, 448, 512)
         for h in range(2):
             nc.vector.tensor_copy(out=y_t[h][:, 256:448], in_=y_b[:, h, :])
         nc.vector.tensor_copy(out=y_t[1][:, 448:512], in_=y_c[1][:])
         nc.scalar.copy(out=y_t[0][:, 448:512], in_=y_c[0][:])
 
-        prod = {}
+        prod = [keep.tile([P, 2, V], F32, name=f"prod{d}") for d in range(D)]
 
         def fetch(h, d):
-            r = keep.tile([P, V], F32, name=f"prod{h}{d}")
-            nc.vector.tensor_tensor(r[:], y_t[h][:].indirect(pos_t[d][:]), gate_t[:, 2 * d + h, :], MULT)
-            prod[h, d] = r[:]
-
-        def add(a, b, name):
-            r = keep.tile([P, V], F32, name=name)
-            nc.vector.tensor_tensor(r[:], a, b, ADD)
-            return r[:]
+            nc.vector.tensor_tensor(
+                prod[d][:, h, :], y_t[h][:].indirect(pos_t[d][:]), gate_t[:, 2 * d + h, :], MULT
+            )
 
         fetch(1, 0)
-        fetch(1, 1)
         fetch(0, 0)
-        part1 = add(prod[1, 0], prod[1, 1], "part1")
+        fetch(1, 1)
         fetch(0, 1)
         fetch(1, 2)
-        part0 = add(prod[0, 0], prod[0, 1], "part0")
+        part = keep.tile([P, 2, V], F32, name="part")
+        nc.vector.tensor_tensor(part[:], prod[0][:], prod[1][:], ADD)
         fetch(0, 2)
-        res1 = add(part1, prod[1, 2], "res1")
-        nc.sync.dma_start(out=out[P : 2 * P, :], in_=res1)
-        res0 = add(part0, prod[0, 2], "res0")
-        nc.sync.dma_start(out=out[0:P, :], in_=res0)
+        res1 = keep.tile([P, V], F32, name="res1")
+        nc.vector.tensor_tensor(res1[:], part[:, 1, :], prod[2][:, 1, :], ADD)
+        nc.sync.dma_start(out=out[P : 2 * P, :], in_=res1[:])
+        for q in range(2):
+            cols = slice(q * V // 2, (q + 1) * V // 2)
+            res0 = keep.tile([P, V // 2], F32, name=f"res0{q}")
+            nc.vector.tensor_tensor(res0[:], part[:, 0, cols], prod[2][:, 0, cols], ADD)
+            nc.sync.dma_start(out=out[0:P, cols], in_=res0[:])

from contextlib import ExitStack

import concourse.mybir as mybir

K, T, D, S, V, H, N = 512, 1024, 3, 512, 256, 512, 256
FLOPS = 2 * S * (K * H + H * N) + 2 * D * N * V

F32 = mybir.dt.float32
BF16 = mybir.dt.bfloat16
U32 = mybir.dt.uint32
U16 = mybir.dt.uint16
U8 = mybir.dt.uint8
FP8X4 = mybir.dt.float8_e4m3fn_x4
SILU = mybir.ActivationFunctionType.Silu
MULT = mybir.AluOpType.mult
ADD = mybir.AluOpType.add

P = 128
PACK = 4


def tile_picked_sub_mlp_silu_sub_e_kernel(tc, xT, w1, w2, gate, offs, pos1, pos2, pos3, out):
    nc = tc.nc
    with ExitStack() as ctx:
        keep = ctx.enter_context(tc.tile_pool(name="keep", bufs=1))
        psum = ctx.enter_context(tc.psum_pool(name="psum", bufs=1))

        offs_t = keep.tile([P, S // 16], U16, name="offs_t")
        pos_t = [keep.tile([P, V // 16], U16, name=f"pos_t{d}") for d in range(D)]

        x_rows = xT.rearrange("(p j) t -> p j t", j=PACK)
        w1_rows = w1.rearrange("(p j) c -> p j c", j=PACK)
        w2_rows = w2.rearrange("(p j) n -> p j n", j=PACK)
        TH = T // 2
        x_raw = {}

        x_raw0 = keep.tile([P, 2, T], F32, name="x_raw0")
        nc.sync.dma_start(out=x_raw0[:], in_=x_rows[:, 0:2, :])
        for h in range(2):
            x_raw[0, h] = x_raw0[:, :, h * TH : (h + 1) * TH]
        nc.sync.dma_start(offs_t[:], offs)
        for h in range(2):
            x_raw1 = keep.tile([P, 2, TH], F32, name=f"x_raw1{h}")
            nc.sync.dma_start(out=x_raw1[:], in_=x_rows[:, 2:4, h * TH : (h + 1) * TH])
            x_raw[1, h] = x_raw1[:]
        W1_CUTS = [(0, 256), (256, 384), (384, 512)]
        w1_raw = []
        for a, b in W1_CUTS:
            r = keep.tile([P, PACK, b - a], F32, name=f"w1_raw{a}")
            nc.sync.dma_start(out=r[:], in_=w1_rows[:, :, a:b])
            w1_raw.append(r)
        w2_raw = keep.tile([P, PACK, N], F32, name="w2_raw")
        nc.sync.dma_start(out=w2_raw[:], in_=w2_rows)
        for d, p in enumerate((pos1, pos2, pos3)):
            nc.sync.dma_start(pos_t[d][:], p)
        gate_t = keep.tile([P, 2 * D, V], F32, name="gate_t")
        nc.sync.dma_start(out=gate_t[:], in_=gate.rearrange("d (h p) v -> p (d h) v", p=P))

        warm = keep.tile([P, 1], F32, name="warm")
        warm_o = keep.tile([P, 1], F32, name="warm_o")
        nc.vector.memset(warm[:], 0.0)
        nc.scalar.activation(warm_o[:], warm[:], SILU)

        x_pair = [keep.tile([P, T, 2], BF16, name=f"x_pair{u}") for u in range(2)]
        X_VECTOR = {(0, 0): 320, (0, 1): 320, (1, 0): 0, (1, 1): 320}

        def cast_x(u, h):
            src = x_raw[u, h].rearrange("p e (c i) -> p c e i", i=4)
            dst = x_pair[u][:, h * TH : (h + 1) * TH, :].rearrange("p (c i) e -> p c e i", i=4)
            cut = X_VECTOR[u, h] // 4
            if cut:
                nc.vector.tensor_copy(out=dst[:, :cut], in_=src[:, :cut])
            nc.scalar.copy(out=dst[:, cut:], in_=src[:, cut:])

        xg = keep.tile([P, S, PACK], BF16, name="xg", align_bytes=64)
        xg_words = xg[:].rearrange("p s t -> p (s t)").bitcast(U32).rearrange("p (s u) -> p s u", u=2)
        x_codes = keep.tile([P, S], U32, name="x_codes", align_bytes=64)
        x_scales = keep.tile([P, S], U8, name="x_scales", align_bytes=64)

        def gather_x(u, a, b):
            window = x_pair[u][:].rearrange("p t e -> p (t e)").bitcast(U32)
            nc.vector.tensor_copy(out=xg_words[:, a:b, u], in_=window.indirect(offs_t[:, a // 16 : b // 16]))

        def quant_x(a, b):
            nc.vector.quantize_mx(
                out=x_codes[:, a:b].bitcast(FP8X4),
                scales=x_scales[:, a:b],
                in_=xg[:, a:b, :].rearrange("p s t -> p (s t)"),
            )

        w1g = keep.tile([P, PACK, P, PACK], BF16, name="w1g", align_bytes=64)
        w1_codes = keep.tile([P, H], U32, name="w1_codes", align_bytes=64)
        w1_scales = keep.tile([P, H], U8, name="w1_scales", align_bytes=64)

        def cast_w1(i, engine_copy, f0, f1):
            a, b = W1_CUTS[i]
            src = w1_raw[i][:].rearrange("p j (m t) -> p m j t", t=PACK)
            n = (b - a) // PACK
            m0, m1 = int(n * f0), int(n * f1)
            engine_copy(
                out=w1g[:].rearrange("p t m j -> p m j t")[:, a // PACK + m0 : a // PACK + m1],
                in_=src[:, m0:m1],
            )

        def quant_w1(half):
            for t in range(PACK):
                m0 = half * 64
                cols = slice(t * P + m0, t * P + m0 + 64)
                nc.vector.quantize_mx(
                    out=w1_codes[:, cols].bitcast(FP8X4),
                    scales=w1_scales[:, cols],
                    in_=w1g[:, t, m0 : m0 + 64, :].rearrange("p m j -> p (m j)"),
                )

        cast_x(0, 0)
        cast_x(0, 1)
        gather_x(0, 0, S)
        cast_x(1, 0)
        cast_x(1, 1)
        gather_x(1, 0, S // 2)
        gather_x(1, S // 2, S)
        cast_w1(0, nc.scalar.copy, 0.0, 1.0)
        cast_w1(1, nc.scalar.copy, 0.0, 1.0)
        quant_w1(0)
        cast_w1(2, nc.vector.tensor_copy, 0.0, 1.0)
        quant_x(0, 128)
        quant_w1(1)
        quant_x(128, 256)
        quant_x(256, 512)

        w2g = keep.tile([P, N, PACK], BF16, name="w2g", align_bytes=64)
        w2_codes = keep.tile([P, N], U32, name="w2_codes", align_bytes=64)
        w2_scales = keep.tile([P, N], U8, name="w2_scales", align_bytes=64)
        nc.vector.tensor_copy(
            out=w2g[:].rearrange("p (c i) j -> p c j i", i=4), in_=w2_raw[:].rearrange("p j (c i) -> p c j i", i=4)
        )
        nc.vector.quantize_mx(
            out=w2_codes[:].bitcast(FP8X4), scales=w2_scales[:], in_=w2g[:].rearrange("p n j -> p (n j)")
        )

        CUTS = [(0, 128), (128, 256), (256, 384), (384, 448), (448, 512)]
        h_codes = keep.tile([P, S], U32, name="h_codes", align_bytes=64)
        h_scales = keep.tile([P, S], U8, name="h_scales", align_bytes=64)
        hg = [keep.tile([P, b - a, PACK], BF16, name=f"hg{a}", align_bytes=64) for a, b in CUTS]
        y_t = [keep.tile([P, S], F32, name=f"y_t{h}") for h in range(2)]

        def layer1(c):
            a, b = CUTS[c]
            ps = psum.tile([P, PACK, b - a], F32, name=f"h_ps{c}", tag=f"h_ps{c % 4}")
            for t in range(PACK):
                nc.tensor.matmul_mx(
                    out=ps[:, t, :],
                    lhsT=w1_codes[:, t * P : (t + 1) * P].bitcast(FP8X4),
                    lhsT_scale=w1_scales[:, t * P : (t + 1) * P],
                    rhs=x_codes[:, a:b].bitcast(FP8X4),
                    rhs_scale=x_scales[:, a:b],
                    start=True,
                    stop=True,
                )
            nc.scalar.activation(hg[c][:], ps[:].rearrange("p t s -> p s t"), SILU)

        def quant_h(c):
            a, b = CUTS[c]
            nc.vector.quantize_mx(
                out=h_codes[:, a:b].bitcast(FP8X4),
                scales=h_scales[:, a:b],
                in_=hg[c][:].rearrange("p s t -> p (s t)"),
            )

        def layer2(dst, h, a, b):
            nc.tensor.matmul_mx(
                out=dst,
                lhsT=w2_codes[:, h * P : (h + 1) * P].bitcast(FP8X4),
                lhsT_scale=w2_scales[:, h * P : (h + 1) * P],
                rhs=h_codes[:, a:b].bitcast(FP8X4),
                rhs_scale=h_scales[:, a:b],
                start=True,
                stop=True,
            )

        for c in range(5):
            layer1(c)
        y_a = psum.tile([P, 2, 256], F32, name="y_a")
        y_b = psum.tile([P, 2, 192], F32, name="y_b")
        y_c = [psum.tile([P, 64], F32, name=f"y_c{h}") for h in range(2)]
        quant_h(0)
        quant_h(1)
        for h in range(2):
            layer2(y_a[:, h, :], h, 0, 256)
        quant_h(2)
        for h in range(2):
            layer2(y_b[:, h, 0:128], h, 256, 384)
        for h in range(2):
            nc.vector.tensor_copy(out=y_t[h][:, 0:256], in_=y_a[:, h, :])
        quant_h(3)
        for h in range(2):
            layer2(y_b[:, h, 128:192], h, 384, 448)
        quant_h(4)
        for h in (1, 0):
            layer2(y_c[h][:], h, 448, 512)
        for h in range(2):
            nc.vector.tensor_copy(out=y_t[h][:, 256:448], in_=y_b[:, h, :])
        nc.vector.tensor_copy(out=y_t[1][:, 448:512], in_=y_c[1][:])
        nc.scalar.copy(out=y_t[0][:, 448:512], in_=y_c[0][:])

        prod = [keep.tile([P, 2, V], F32, name=f"prod{d}") for d in range(D)]

        def fetch(h, d):
            nc.vector.tensor_tensor(
                prod[d][:, h, :], y_t[h][:].indirect(pos_t[d][:]), gate_t[:, 2 * d + h, :], MULT
            )

        fetch(1, 0)
        fetch(0, 0)
        fetch(1, 1)
        fetch(0, 1)
        fetch(1, 2)
        part = keep.tile([P, 2, V], F32, name="part")
        nc.vector.tensor_tensor(part[:], prod[0][:], prod[1][:], ADD)
        fetch(0, 2)
        res1 = keep.tile([P, V], F32, name="res1")
        nc.vector.tensor_tensor(res1[:], part[:, 1, :], prod[2][:, 1, :], ADD)
        nc.sync.dma_start(out=out[P : 2 * P, :], in_=res1[:])
        for q in range(2):
            cols = slice(q * V // 2, (q + 1) * V // 2)
            res0 = keep.tile([P, V // 2], F32, name=f"res0{q}")
            nc.vector.tensor_tensor(res0[:], part[:, 0, cols], prod[2][:, 0, cols], ADD)
            nc.sync.dma_start(out=out[0:P, cols], in_=res0[:])
